import numpy as np
import ml_dtypes

BF16 = ml_dtypes.bfloat16


def bf(x):
    return np.asarray(x, np.float32).astype(BF16)


def f32(x):
    return np.asarray(x, np.float32)


def f64(x):
    return np.asarray(x).astype(np.float64)


def striped(idx):
    return np.tile(idx.reshape(-1, 16).T, (8, 1))


S, K, M, N, D, V = 1024, 256, 128, 384, 3, 128


def setup_inputs():
    return {"table": bf(np.random.standard_normal((S, K))), "w": bf(np.random.standard_normal((D, K, M)) / np.sqrt(D * K)), "c": f32(0.2 + 0.8 * np.random.random_sample((1, V))), "offs": striped(np.random.permutation(S)[:N])}


def reference(table, w, c, offs):
    idx = offs[:16].T.reshape(-1)
    x = f64(table)[idx].T
    y = sum(f64(w)[t].T @ x[:, t * V : (t + 1) * V] for t in range(D))
    return y * f64(c)

@@ -1,0 +1,61 @@
+import concourse.mybir as mybir
+from concourse.masks import make_identity
+
+BF16, F32, U16 = mybir.dt.bfloat16, mybir.dt.float32, mybir.dt.uint16
+
+P = 128
+S, K = 1024, 256
+D, M, V = 3, 128, 128
+N = D * V
+NODE_BLOCKS = S // P
+FEATURE_BLOCKS = K // P
+LIST_COLUMNS = V // 16
+
+FLOPS = 2 * D * K * M * V
+
+
+def tile_gather_matmul_kernel(tc, table, w, c, offs, out):
+    nc = tc.nc
+    with (
+        tc.tile_pool(name="held", bufs=1) as held,
+        tc.psum_pool(name="flip", bufs=3) as flip,
+        tc.psum_pool(name="sums", bufs=1) as sums,
+    ):
+        offsets = held.tile([P, N // 16], U16, name="offsets")
+        nc.sync.dma_start(offsets[:], offs)
+
+        rows = [held.tile([P, K], BF16, name=f"rows{a}") for a in range(NODE_BLOCKS)]
+        for a in range(NODE_BLOCKS):
+            queue = nc.sync if a % 2 == 0 else nc.scalar
+            queue.dma_start(rows[a][:], table[a * P : (a + 1) * P, :])
+
+        weights = held.tile([P, D, FEATURE_BLOCKS, M], BF16, name="weights")
+        nc.gpsimd.dma_start(weights[:], w.rearrange("t (b p) m -> p t b m", p=P))
+
+        c_all = held.tile([P, V], F32, name="c_all")
+        nc.gpsimd.dma_start(c_all[:], c.broadcast_to([P, V]))
+
+        identity = held.tile([P, P], BF16, name="identity")
+        make_identity(nc, identity[:])
+
+        window = [held.tile([P, S], BF16, name=f"window{b}") for b in range(FEATURE_BLOCKS)]
+        for a in range(NODE_BLOCKS):
+            for b in range(FEATURE_BLOCKS):
+                flipped = flip.tile([P, P], BF16, name=f"flipped{b}")
+                nc.tensor.transpose(flipped[:], rows[a][:, b * P : (b + 1) * P], identity[:])
+                if b == 0:
+                    nc.vector.tensor_copy(window[b][:, a * P : (a + 1) * P], flipped[:])
+                else:
+                    nc.scalar.copy(window[b][:, a * P : (a + 1) * P], flipped[:])
+
+        y = sums.tile([M, V], F32, name="y")
+        passes = [(b, t) for b in range(FEATURE_BLOCKS) for t in range(D)]
+        for i, (b, t) in enumerate(passes):
+            picked = window[b][:].indirect(offsets[:, t * LIST_COLUMNS : (t + 1) * LIST_COLUMNS])
+            nc.tensor.matmul(
+                y[:], weights[:, t, b, :], picked, start=(i == 0), stop=(i == len(passes) - 1)
+            )
+
+        scaled = held.tile([M, V], F32, name="scaled")
+        nc.vector.tensor_tensor(scaled[:], y[:], c_all[:], mybir.AluOpType.mult)
+        nc.sync.dma_start(out, scaled[:])

@@ -10,6 +10,7 @@ N = D * V
 NODE_BLOCKS = S // P
 FEATURE_BLOCKS = K // P
 LIST_COLUMNS = V // 16
+PAIR = 2
 
 FLOPS = 2 * D * K * M * V
 
@@ -18,42 +19,53 @@ def tile_gather_matmul_kernel(tc, table, w, c, offs, out):
     nc = tc.nc
     with (
         tc.tile_pool(name="held", bufs=1) as held,
-        tc.psum_pool(name="flip", bufs=3) as flip,
+        tc.psum_pool(name="flip", bufs=4) as flip,
         tc.psum_pool(name="sums", bufs=1) as sums,
     ):
-        offsets = held.tile([P, N // 16], U16, name="offsets")
-        nc.sync.dma_start(offsets[:], offs)
+        c_row = held.tile([1, V], F32, name="c_row")
+        nc.scalar.dma_start(c_row[:], c)
 
         rows = [held.tile([P, K], BF16, name=f"rows{a}") for a in range(NODE_BLOCKS)]
         for a in range(NODE_BLOCKS):
             queue = nc.sync if a % 2 == 0 else nc.scalar
             queue.dma_start(rows[a][:], table[a * P : (a + 1) * P, :])
 
-        weights = held.tile([P, D, FEATURE_BLOCKS, M], BF16, name="weights")
-        nc.gpsimd.dma_start(weights[:], w.rearrange("t (b p) m -> p t b m", p=P))
+        offsets = held.tile([P, N // 16], U16, name="offsets")
+        nc.sync.dma_start(offsets[:], offs)
 
-        c_all = held.tile([P, V], F32, name="c_all")
-        nc.gpsimd.dma_start(c_all[:], c.broadcast_to([P, V]))
+        weights = [held.tile([P, D, M], BF16, name=f"weights{b}") for b in range(FEATURE_BLOCKS)]
+        for b in range(FEATURE_BLOCKS):
+            queue = nc.sync if b % 2 == 0 else nc.scalar
+            queue.dma_start(weights[b][:], w[:, b * P : (b + 1) * P, :].rearrange("t p m -> p t m"))
 
         identity = held.tile([P, P], BF16, name="identity")
         make_identity(nc, identity[:])
 
+        ones = held.tile([1, P], F32, name="ones")
+        nc.vector.memset(ones[:], 1.0)
+        c_spread = sums.tile([P, V], F32, name="c_spread")
+        nc.tensor.matmul(c_spread[:], ones[:], c_row[:], start=True, stop=True)
+        c_all = held.tile([P, V], F32, name="c_all")
+        nc.vector.tensor_copy(c_all[:], c_spread[:])
+
         window = [held.tile([P, S], BF16, name=f"window{b}") for b in range(FEATURE_BLOCKS)]
-        for a in range(NODE_BLOCKS):
+        for g in range(NODE_BLOCKS // PAIR):
             for b in range(FEATURE_BLOCKS):
-                flipped = flip.tile([P, P], BF16, name=f"flipped{b}")
-                nc.tensor.transpose(flipped[:], rows[a][:, b * P : (b + 1) * P], identity[:])
-                if b == 0:
-                    nc.vector.tensor_copy(window[b][:, a * P : (a + 1) * P], flipped[:])
-                else:
-                    nc.scalar.copy(window[b][:, a * P : (a + 1) * P], flipped[:])
+                flipped = flip.tile([P, PAIR * P], BF16, name="flipped")
+                for j in range(PAIR):
+                    nc.tensor.transpose(
+                        flipped[:, j * P : (j + 1) * P],
+                        rows[g * PAIR + j][:, b * P : (b + 1) * P],
+                        identity[:],
+                    )
+                nc.vector.tensor_copy(window[b][:, g * PAIR * P : (g + 1) * PAIR * P], flipped[:])
 
         y = sums.tile([M, V], F32, name="y")
         passes = [(b, t) for b in range(FEATURE_BLOCKS) for t in range(D)]
         for i, (b, t) in enumerate(passes):
             picked = window[b][:].indirect(offsets[:, t * LIST_COLUMNS : (t + 1) * LIST_COLUMNS])
             nc.tensor.matmul(
-                y[:], weights[:, t, b, :], picked, start=(i == 0), stop=(i == len(passes) - 1)
+                y[:], weights[b][:, t, :], picked, start=(i == 0), stop=(i == len(passes) - 1)
             )
 
         scaled = held.tile([M, V], F32, name="scaled")

@@ -11,6 +11,8 @@ NODE_BLOCKS = S // P
 FEATURE_BLOCKS = K // P
 LIST_COLUMNS = V // 16
 PAIR = 2
+WARM_UP = 4
+BANK = 512
 
 FLOPS = 2 * D * K * M * V
 
@@ -40,6 +42,12 @@ def tile_gather_matmul_kernel(tc, table, w, c, offs, out):
 
         identity = held.tile([P, P], BF16, name="identity")
         make_identity(nc, identity[:])
+
+        zeros = held.tile([P, BANK], BF16, name="zeros")
+        nc.vector.memset(zeros[:], 0.0)
+        unread = sums.tile([P, BANK], F32, name="unread")
+        for i in range(WARM_UP):
+            nc.tensor.matmul(unread[:], zeros[:, 0:P], zeros[:], start=True, stop=True)
 
         ones = held.tile([1, P], F32, name="ones")
         nc.vector.memset(ones[:], 1.0)

@@ -11,8 +11,7 @@ NODE_BLOCKS = S // P
 FEATURE_BLOCKS = K // P
 LIST_COLUMNS = V // 16
 PAIR = 2
-WARM_UP = 4
-BANK = 512
+WARM_UP = 12
 
 FLOPS = 2 * D * K * M * V
 
@@ -24,6 +23,12 @@ def tile_gather_matmul_kernel(tc, table, w, c, offs, out):
         tc.psum_pool(name="flip", bufs=4) as flip,
         tc.psum_pool(name="sums", bufs=1) as sums,
     ):
+        zeros = held.tile([P, P], BF16, name="zeros")
+        nc.vector.memset(zeros[:], 0.0)
+        unread = sums.tile([P, P], F32, name="unread")
+        for i in range(WARM_UP):
+            nc.tensor.matmul(unread[:], zeros[:], zeros[:], start=True, stop=True)
+
         c_row = held.tile([1, V], F32, name="c_row")
         nc.scalar.dma_start(c_row[:], c)
 
@@ -42,12 +47,6 @@ def tile_gather_matmul_kernel(tc, table, w, c, offs, out):
 
         identity = held.tile([P, P], BF16, name="identity")
         make_identity(nc, identity[:])
-
-        zeros = held.tile([P, BANK], BF16, name="zeros")
-        nc.vector.memset(zeros[:], 0.0)
-        unread = sums.tile([P, BANK], F32, name="unread")
-        for i in range(WARM_UP):
-            nc.tensor.matmul(unread[:], zeros[:, 0:P], zeros[:], start=True, stop=True)
 
         ones = held.tile([1, P], F32, name="ones")
         nc.vector.memset(ones[:], 1.0)

@@ -7,11 +7,11 @@ P = 128
 S, K = 1024, 256
 D, M, V = 3, 128, 128
 N = D * V
-NODE_BLOCKS = S // P
-FEATURE_BLOCKS = K // P
 LIST_COLUMNS = V // 16
-PAIR = 2
-WARM_UP = 12
+NODE_BLOCKS = S // P
+GROUP = 2
+PACK = 2
+assert K == PACK * P
 
 FLOPS = 2 * D * K * M * V
 
@@ -20,15 +20,11 @@ def tile_gather_matmul_kernel(tc, table, w, c, offs, out):
     nc = tc.nc
     with (
         tc.tile_pool(name="held", bufs=1) as held,
-        tc.psum_pool(name="flip", bufs=4) as flip,
+        tc.psum_pool(name="flip", bufs=NODE_BLOCKS // GROUP) as flip,
         tc.psum_pool(name="sums", bufs=1) as sums,
     ):
-        zeros = held.tile([P, P], BF16, name="zeros")
-        nc.vector.memset(zeros[:], 0.0)
-        unread = sums.tile([P, P], F32, name="unread")
-        for i in range(WARM_UP):
-            nc.tensor.matmul(unread[:], zeros[:], zeros[:], start=True, stop=True)
-
+        offsets = held.tile([P, N // 16], U16, name="offsets")
+        nc.sync.dma_start(offsets[:], offs)
         c_row = held.tile([1, V], F32, name="c_row")
         nc.scalar.dma_start(c_row[:], c)
 
@@ -37,15 +33,10 @@ def tile_gather_matmul_kernel(tc, table, w, c, offs, out):
             queue = nc.sync if a % 2 == 0 else nc.scalar
             queue.dma_start(rows[a][:], table[a * P : (a + 1) * P, :])
 
-        offsets = held.tile([P, N // 16], U16, name="offsets")
-        nc.sync.dma_start(offsets[:], offs)
+        weights = held.tile([P, D, PACK, M], BF16, name="weights")
+        nc.sync.dma_start(weights[:], w.rearrange("t (p e) m -> p t e m", e=PACK))
 
-        weights = [held.tile([P, D, M], BF16, name=f"weights{b}") for b in range(FEATURE_BLOCKS)]
-        for b in range(FEATURE_BLOCKS):
-            queue = nc.sync if b % 2 == 0 else nc.scalar
-            queue.dma_start(weights[b][:], w[:, b * P : (b + 1) * P, :].rearrange("t p m -> p t m"))
-
-        identity = held.tile([P, P], BF16, name="identity")
+        identity = held.tile([P, P], F32, name="identity")
         make_identity(nc, identity[:])
 
         ones = held.tile([1, P], F32, name="ones")
@@ -55,24 +46,23 @@ def tile_gather_matmul_kernel(tc, table, w, c, offs, out):
         c_all = held.tile([P, V], F32, name="c_all")
         nc.vector.tensor_copy(c_all[:], c_spread[:])
 
-        window = [held.tile([P, S], BF16, name=f"window{b}") for b in range(FEATURE_BLOCKS)]
-        for g in range(NODE_BLOCKS // PAIR):
-            for b in range(FEATURE_BLOCKS):
-                flipped = flip.tile([P, PAIR * P], BF16, name="flipped")
-                for j in range(PAIR):
-                    nc.tensor.transpose(
-                        flipped[:, j * P : (j + 1) * P],
-                        rows[g * PAIR + j][:, b * P : (b + 1) * P],
-                        identity[:],
-                    )
-                nc.vector.tensor_copy(window[b][:, g * PAIR * P : (g + 1) * PAIR * P], flipped[:])
+        window = [held.tile([P, S], BF16, name=f"window{e}") for e in range(PACK)]
+        for g in range(NODE_BLOCKS // GROUP):
+            flipped = flip.tile([P, GROUP * P], F32, name="flipped")
+            for j in range(GROUP):
+                nc.tensor.transpose(
+                    flipped[:, j * P : (j + 1) * P], rows[g * GROUP + j][:].bitcast(F32), identity[:]
+                )
+            halves = flipped[:].bitcast(BF16).rearrange("p (n e) -> p e n", e=PACK)
+            nc.vector.tensor_copy(window[0][:, g * GROUP * P : (g + 1) * GROUP * P], halves[:, 0, :])
+            nc.scalar.copy(window[1][:, g * GROUP * P : (g + 1) * GROUP * P], halves[:, 1, :])
 
         y = sums.tile([M, V], F32, name="y")
-        passes = [(b, t) for b in range(FEATURE_BLOCKS) for t in range(D)]
-        for i, (b, t) in enumerate(passes):
-            picked = window[b][:].indirect(offsets[:, t * LIST_COLUMNS : (t + 1) * LIST_COLUMNS])
+        passes = [(e, t) for e in range(PACK) for t in range(D)]
+        for i, (e, t) in enumerate(passes):
+            picked = window[e][:].indirect(offsets[:, t * LIST_COLUMNS : (t + 1) * LIST_COLUMNS])
             nc.tensor.matmul(
-                y[:], weights[b][:, t, :], picked, start=(i == 0), stop=(i == len(passes) - 1)
+                y[:], weights[:, t, e, :], picked, start=(i == 0), stop=(i == len(passes) - 1)
             )
 
         scaled = held.tile([M, V], F32, name="scaled")

@@ -8,8 +8,9 @@ S, K = 1024, 256
 D, M, V = 3, 128, 128
 N = D * V
 LIST_COLUMNS = V // 16
-NODE_BLOCKS = S // P
-GROUP = 2
+PAIR = 2
+QUARTER = PAIR * P
+LOADS = S // QUARTER
 PACK = 2
 assert K == PACK * P
 
@@ -20,7 +21,7 @@ def tile_gather_matmul_kernel(tc, table, w, c, offs, out):
     nc = tc.nc
     with (
         tc.tile_pool(name="held", bufs=1) as held,
-        tc.psum_pool(name="flip", bufs=NODE_BLOCKS // GROUP) as flip,
+        tc.psum_pool(name="flip", bufs=LOADS) as flip,
         tc.psum_pool(name="sums", bufs=1) as sums,
     ):
         offsets = held.tile([P, N // 16], U16, name="offsets")
@@ -28,10 +29,13 @@ def tile_gather_matmul_kernel(tc, table, w, c, offs, out):
         c_row = held.tile([1, V], F32, name="c_row")
         nc.scalar.dma_start(c_row[:], c)
 
-        rows = [held.tile([P, K], BF16, name=f"rows{a}") for a in range(NODE_BLOCKS)]
-        for a in range(NODE_BLOCKS):
-            queue = nc.sync if a % 2 == 0 else nc.scalar
-            queue.dma_start(rows[a][:], table[a * P : (a + 1) * P, :])
+        rows = [held.tile([P, PAIR * K], BF16, name=f"rows{q}") for q in range(LOADS)]
+        for q in range(LOADS):
+            queue = nc.sync if q % 2 == 0 else nc.scalar
+            queue.dma_start(
+                rows[q][:],
+                table[q * QUARTER : (q + 1) * QUARTER, :].rearrange("(p a) k -> p (a k)", a=PAIR),
+            )
 
         weights = held.tile([P, D, PACK, M], BF16, name="weights")
         nc.sync.dma_start(weights[:], w.rearrange("t (p e) m -> p t e m", e=PACK))
@@ -47,15 +51,21 @@ def tile_gather_matmul_kernel(tc, table, w, c, offs, out):
         nc.vector.tensor_copy(c_all[:], c_spread[:])
 
         window = [held.tile([P, S], BF16, name=f"window{e}") for e in range(PACK)]
-        for g in range(NODE_BLOCKS // GROUP):
-            flipped = flip.tile([P, GROUP * P], F32, name="flipped")
-            for j in range(GROUP):
+        for q in range(LOADS):
+            words = rows[q][:].bitcast(F32)
+            flipped = flip.tile([P, PAIR * P], F32, name="flipped")
+            for a in range(PAIR):
                 nc.tensor.transpose(
-                    flipped[:, j * P : (j + 1) * P], rows[g * GROUP + j][:].bitcast(F32), identity[:]
+                    flipped[:, a * P : (a + 1) * P], words[:, a * P : (a + 1) * P], identity[:]
                 )
-            halves = flipped[:].bitcast(BF16).rearrange("p (n e) -> p e n", e=PACK)
-            nc.vector.tensor_copy(window[0][:, g * GROUP * P : (g + 1) * GROUP * P], halves[:, 0, :])
-            nc.scalar.copy(window[1][:, g * GROUP * P : (g + 1) * GROUP * P], halves[:, 1, :])
+            halves = flipped[:].bitcast(BF16).rearrange("p (a n e) -> p e n a", a=PAIR, e=PACK)
+            columns = slice(q * QUARTER, (q + 1) * QUARTER)
+            nc.vector.tensor_copy(
+                window[0][:, columns].rearrange("p (n a) -> p n a", a=PAIR), halves[:, 0, :, :]
+            )
+            nc.scalar.copy(
+                window[1][:, columns].rearrange("p (n a) -> p n a", a=PAIR), halves[:, 1, :, :]
+            )
 
         y = sums.tile([M, V], F32, name="y")
         passes = [(e, t) for e in range(PACK) for t in range(D)]

@@ -51,6 +51,7 @@ def tile_gather_matmul_kernel(tc, table, w, c, offs, out):
         nc.vector.tensor_copy(c_all[:], c_spread[:])
 
         window = [held.tile([P, S], BF16, name=f"window{e}") for e in range(PACK)]
+        halves = []
         for q in range(LOADS):
             words = rows[q][:].bitcast(F32)
             flipped = flip.tile([P, PAIR * P], F32, name="flipped")
@@ -58,14 +59,12 @@ def tile_gather_matmul_kernel(tc, table, w, c, offs, out):
                 nc.tensor.transpose(
                     flipped[:, a * P : (a + 1) * P], words[:, a * P : (a + 1) * P], identity[:]
                 )
-            halves = flipped[:].bitcast(BF16).rearrange("p (a n e) -> p e n a", a=PAIR, e=PACK)
-            columns = slice(q * QUARTER, (q + 1) * QUARTER)
-            nc.vector.tensor_copy(
-                window[0][:, columns].rearrange("p (n a) -> p n a", a=PAIR), halves[:, 0, :, :]
-            )
-            nc.scalar.copy(
-                window[1][:, columns].rearrange("p (n a) -> p n a", a=PAIR), halves[:, 1, :, :]
-            )
+            halves.append(flipped[:].bitcast(BF16).rearrange("p (a n e) -> p e n a", a=PAIR, e=PACK))
+        for e in range(PACK):
+            for q in range(LOADS):
+                copy = nc.vector.tensor_copy if q % 2 == 0 else nc.scalar.copy
+                columns = window[e][:, q * QUARTER : (q + 1) * QUARTER]
+                copy(columns.rearrange("p (n a) -> p n a", a=PAIR), halves[q][:, e, :, :])
 
         y = sums.tile([M, V], F32, name="y")
         passes = [(e, t) for e in range(PACK) for t in range(D)]

@@ -13,6 +13,7 @@ QUARTER = PAIR * P
 LOADS = S // QUARTER
 PACK = 2
 assert K == PACK * P
+WARM_UP = 16
 
 FLOPS = 2 * D * K * M * V
 
@@ -24,6 +25,12 @@ def tile_gather_matmul_kernel(tc, table, w, c, offs, out):
         tc.psum_pool(name="flip", bufs=LOADS) as flip,
         tc.psum_pool(name="sums", bufs=1) as sums,
     ):
+        zeros = held.tile([P, P], BF16, name="zeros")
+        nc.vector.memset(zeros[:], 0.0)
+        unread = sums.tile([P, P], F32, name="unread")
+        for i in range(WARM_UP):
+            nc.tensor.matmul(unread[:], zeros[:], zeros[:], start=True, stop=True)
+
         offsets = held.tile([P, N // 16], U16, name="offsets")
         nc.sync.dma_start(offsets[:], offs)
         c_row = held.tile([1, V], F32, name="c_row")

@@ -13,7 +13,7 @@ QUARTER = PAIR * P
 LOADS = S // QUARTER
 PACK = 2
 assert K == PACK * P
-WARM_UP = 16
+WARM_UP = 10
 
 FLOPS = 2 * D * K * M * V
 

@@ -38,7 +38,7 @@ def tile_gather_matmul_kernel(tc, table, w, c, offs, out):
 
         rows = [held.tile([P, PAIR * K], BF16, name=f"rows{q}") for q in range(LOADS)]
         for q in range(LOADS):
-            queue = nc.sync if q % 2 == 0 else nc.scalar
+            queue = nc.scalar if q % 2 == 0 else nc.sync
             queue.dma_start(
                 rows[q][:],
                 table[q * QUARTER : (q + 1) * QUARTER, :].rearrange("(p a) k -> p (a k)", a=PAIR),

@@ -58,7 +58,6 @@ def tile_gather_matmul_kernel(tc, table, w, c, offs, out):
         nc.vector.tensor_copy(c_all[:], c_spread[:])
 
         window = [held.tile([P, S], BF16, name=f"window{e}") for e in range(PACK)]
-        halves = []
         for q in range(LOADS):
             words = rows[q][:].bitcast(F32)
             flipped = flip.tile([P, PAIR * P], F32, name="flipped")
@@ -66,12 +65,11 @@ def tile_gather_matmul_kernel(tc, table, w, c, offs, out):
                 nc.tensor.transpose(
                     flipped[:, a * P : (a + 1) * P], words[:, a * P : (a + 1) * P], identity[:]
                 )
-            halves.append(flipped[:].bitcast(BF16).rearrange("p (a n e) -> p e n a", a=PAIR, e=PACK))
-        for e in range(PACK):
-            for q in range(LOADS):
-                copy = nc.vector.tensor_copy if q % 2 == 0 else nc.scalar.copy
+            halves = flipped[:].bitcast(BF16).rearrange("p (a n e) -> p e n a", a=PAIR, e=PACK)
+            copy = nc.vector.tensor_copy if q % 2 == 0 else nc.scalar.copy
+            for e in range(PACK):
                 columns = window[e][:, q * QUARTER : (q + 1) * QUARTER]
-                copy(columns.rearrange("p (n a) -> p n a", a=PAIR), halves[q][:, e, :, :])
+                copy(columns.rearrange("p (n a) -> p n a", a=PAIR), halves[:, e, :, :])
 
         y = sums.tile([M, V], F32, name="y")
         passes = [(e, t) for e in range(PACK) for t in range(D)]

@@ -31,31 +31,23 @@ def tile_gather_matmul_kernel(tc, table, w, c, offs, out):
         for i in range(WARM_UP):
             nc.tensor.matmul(unread[:], zeros[:], zeros[:], start=True, stop=True)
 
-        offsets = held.tile([P, N // 16], U16, name="offsets")
-        nc.sync.dma_start(offsets[:], offs)
-        c_row = held.tile([1, V], F32, name="c_row")
-        nc.scalar.dma_start(c_row[:], c)
-
         rows = [held.tile([P, PAIR * K], BF16, name=f"rows{q}") for q in range(LOADS)]
         for q in range(LOADS):
-            queue = nc.scalar if q % 2 == 0 else nc.sync
+            queue = nc.sync if q % 2 == 0 else nc.scalar
             queue.dma_start(
                 rows[q][:],
                 table[q * QUARTER : (q + 1) * QUARTER, :].rearrange("(p a) k -> p (a k)", a=PAIR),
             )
 
+        offsets = held.tile([P, N // 16], U16, name="offsets")
+        nc.sync.dma_start(offsets[:], offs)
+        c_row = held.tile([1, V], F32, name="c_row")
+        nc.scalar.dma_start(c_row[:], c)
         weights = held.tile([P, D, PACK, M], BF16, name="weights")
-        nc.sync.dma_start(weights[:], w.rearrange("t (p e) m -> p t e m", e=PACK))
+        nc.scalar.dma_start(weights[:], w.rearrange("t (p e) m -> p t e m", e=PACK))
 
         identity = held.tile([P, P], F32, name="identity")
         make_identity(nc, identity[:])
-
-        ones = held.tile([1, P], F32, name="ones")
-        nc.vector.memset(ones[:], 1.0)
-        c_spread = sums.tile([P, V], F32, name="c_spread")
-        nc.tensor.matmul(c_spread[:], ones[:], c_row[:], start=True, stop=True)
-        c_all = held.tile([P, V], F32, name="c_all")
-        nc.vector.tensor_copy(c_all[:], c_spread[:])
 
         window = [held.tile([P, S], BF16, name=f"window{e}") for e in range(PACK)]
         for q in range(LOADS):
@@ -70,6 +62,13 @@ def tile_gather_matmul_kernel(tc, table, w, c, offs, out):
             for e in range(PACK):
                 columns = window[e][:, q * QUARTER : (q + 1) * QUARTER]
                 copy(columns.rearrange("p (n a) -> p n a", a=PAIR), halves[:, e, :, :])
+
+        ones = held.tile([1, P], F32, name="ones")
+        nc.vector.memset(ones[:], 1.0)
+        c_spread = flip.tile([P, PAIR * P], F32, name="c_spread", tag="flipped")
+        nc.tensor.matmul(c_spread[:, :V], ones[:], c_row[:], start=True, stop=True)
+        c_all = held.tile([P, V], F32, name="c_all")
+        nc.vector.tensor_copy(c_all[:], c_spread[:, :V])
 
         y = sums.tile([M, V], F32, name="y")
         passes = [(e, t) for e in range(PACK) for t in range(D)]

@@ -13,6 +13,7 @@ QUARTER = PAIR * P
 LOADS = S // QUARTER
 PACK = 2
 assert K == PACK * P
+LAST = LOADS - 1
 WARM_UP = 10
 
 FLOPS = 2 * D * K * M * V
@@ -22,7 +23,8 @@ def tile_gather_matmul_kernel(tc, table, w, c, offs, out):
     nc = tc.nc
     with (
         tc.tile_pool(name="held", bufs=1) as held,
-        tc.psum_pool(name="flip", bufs=LOADS) as flip,
+        tc.psum_pool(name="flip", bufs=LAST) as flip,
+        tc.psum_pool(name="flip_last", bufs=PACK) as flip_last,
         tc.psum_pool(name="sums", bufs=1) as sums,
     ):
         zeros = held.tile([P, P], BF16, name="zeros")
@@ -31,12 +33,12 @@ def tile_gather_matmul_kernel(tc, table, w, c, offs, out):
         for i in range(WARM_UP):
             nc.tensor.matmul(unread[:], zeros[:], zeros[:], start=True, stop=True)
 
-        rows = [held.tile([P, PAIR * K], BF16, name=f"rows{q}") for q in range(LOADS)]
+        rows = [held.tile([P, PAIR, K], BF16, name=f"rows{q}") for q in range(LOADS)]
         for q in range(LOADS):
             queue = nc.sync if q % 2 == 0 else nc.scalar
+            nodes = "(p a) k -> p a k" if q < LAST else "(a p) k -> p a k"
             queue.dma_start(
-                rows[q][:],
-                table[q * QUARTER : (q + 1) * QUARTER, :].rearrange("(p a) k -> p (a k)", a=PAIR),
+                rows[q][:], table[q * QUARTER : (q + 1) * QUARTER, :].rearrange(nodes, a=PAIR)
             )
 
         offsets = held.tile([P, N // 16], U16, name="offsets")
@@ -48,20 +50,31 @@ def tile_gather_matmul_kernel(tc, table, w, c, offs, out):
 
         identity = held.tile([P, P], F32, name="identity")
         make_identity(nc, identity[:])
+        identity_bf16 = held.tile([P, P], BF16, name="identity_bf16")
+        make_identity(nc, identity_bf16[:])
 
         window = [held.tile([P, S], BF16, name=f"window{e}") for e in range(PACK)]
-        for q in range(LOADS):
+        for q in range(LAST):
             words = rows[q][:].bitcast(F32)
             flipped = flip.tile([P, PAIR * P], F32, name="flipped")
             for a in range(PAIR):
                 nc.tensor.transpose(
-                    flipped[:, a * P : (a + 1) * P], words[:, a * P : (a + 1) * P], identity[:]
+                    flipped[:, a * P : (a + 1) * P], words[:, a, :], identity[:]
                 )
             halves = flipped[:].bitcast(BF16).rearrange("p (a n e) -> p e n a", a=PAIR, e=PACK)
             copy = nc.vector.tensor_copy if q % 2 == 0 else nc.scalar.copy
             for e in range(PACK):
                 columns = window[e][:, q * QUARTER : (q + 1) * QUARTER]
                 copy(columns.rearrange("p (n a) -> p n a", a=PAIR), halves[:, e, :, :])
+
+        for e in range(PACK):
+            features = rows[LAST][:].rearrange("p a (k e) -> p a e k", e=PACK)
+            flipped_last = flip_last.tile([P, QUARTER], BF16, name="flipped_last")
+            for a in range(PAIR):
+                nc.tensor.transpose(
+                    flipped_last[:, a * P : (a + 1) * P], features[:, a, e, :], identity_bf16[:]
+                )
+            nc.scalar.copy(window[e][:, LAST * QUARTER :], flipped_last[:])
 
         ones = held.tile([1, P], F32, name="ones")
         nc.vector.memset(ones[:], 1.0)

import concourse.mybir as mybir
from concourse.masks import make_identity

BF16, F32, U16 = mybir.dt.bfloat16, mybir.dt.float32, mybir.dt.uint16

P = 128
S, K = 1024, 256
D, M, V = 3, 128, 128
N = D * V
LIST_COLUMNS = V // 16
PAIR = 2
QUARTER = PAIR * P
LOADS = S // QUARTER
PACK = 2
assert K == PACK * P
LAST = LOADS - 1
WARM_UP = 10

FLOPS = 2 * D * K * M * V


def tile_gather_matmul_kernel(tc, table, w, c, offs, out):
    nc = tc.nc
    with (
        tc.tile_pool(name="held", bufs=1) as held,
        tc.psum_pool(name="flip", bufs=LAST) as flip,
        tc.psum_pool(name="flip_last", bufs=PACK) as flip_last,
        tc.psum_pool(name="sums", bufs=1) as sums,
    ):
        zeros = held.tile([P, P], BF16, name="zeros")
        nc.vector.memset(zeros[:], 0.0)
        unread = sums.tile([P, P], F32, name="unread")
        for i in range(WARM_UP):
            nc.tensor.matmul(unread[:], zeros[:], zeros[:], start=True, stop=True)

        rows = [held.tile([P, PAIR, K], BF16, name=f"rows{q}") for q in range(LOADS)]
        for q in range(LOADS):
            queue = nc.sync if q % 2 == 0 else nc.scalar
            nodes = "(p a) k -> p a k" if q < LAST else "(a p) k -> p a k"
            queue.dma_start(
                rows[q][:], table[q * QUARTER : (q + 1) * QUARTER, :].rearrange(nodes, a=PAIR)
            )

        offsets = held.tile([P, N // 16], U16, name="offsets")
        nc.sync.dma_start(offsets[:], offs)
        c_row = held.tile([1, V], F32, name="c_row")
        nc.scalar.dma_start(c_row[:], c)
        weights = held.tile([P, D, PACK, M], BF16, name="weights")
        nc.scalar.dma_start(weights[:], w.rearrange("t (p e) m -> p t e m", e=PACK))

        identity = held.tile([P, P], F32, name="identity")
        make_identity(nc, identity[:])
        identity_bf16 = held.tile([P, P], BF16, name="identity_bf16")
        make_identity(nc, identity_bf16[:])

        window = [held.tile([P, S], BF16, name=f"window{e}") for e in range(PACK)]
        for q in range(LAST):
            words = rows[q][:].bitcast(F32)
            flipped = flip.tile([P, PAIR * P], F32, name="flipped")
            for a in range(PAIR):
                nc.tensor.transpose(
                    flipped[:, a * P : (a + 1) * P], words[:, a, :], identity[:]
                )
            halves = flipped[:].bitcast(BF16).rearrange("p (a n e) -> p e n a", a=PAIR, e=PACK)
            copy = nc.vector.tensor_copy if q % 2 == 0 else nc.scalar.copy
            for e in range(PACK):
                columns = window[e][:, q * QUARTER : (q + 1) * QUARTER]
                copy(columns.rearrange("p (n a) -> p n a", a=PAIR), halves[:, e, :, :])

        for e in range(PACK):
            features = rows[LAST][:].rearrange("p a (k e) -> p a e k", e=PACK)
            flipped_last = flip_last.tile([P, QUARTER], BF16, name="flipped_last")
            for a in range(PAIR):
                nc.tensor.transpose(
                    flipped_last[:, a * P : (a + 1) * P], features[:, a, e, :], identity_bf16[:]
                )
            nc.scalar.copy(window[e][:, LAST * QUARTER :], flipped_last[:])

        ones = held.tile([1, P], F32, name="ones")
        nc.vector.memset(ones[:], 1.0)
        c_spread = flip.tile([P, PAIR * P], F32, name="c_spread", tag="flipped")
        nc.tensor.matmul(c_spread[:, :V], ones[:], c_row[:], start=True, stop=True)
        c_all = held.tile([P, V], F32, name="c_all")
        nc.vector.tensor_copy(c_all[:], c_spread[:, :V])

        y = sums.tile([M, V], F32, name="y")
        passes = [(e, t) for e in range(PACK) for t in range(D)]
        for i, (e, t) in enumerate(passes):
            picked = window[e][:].indirect(offsets[:, t * LIST_COLUMNS : (t + 1) * LIST_COLUMNS])
            nc.tensor.matmul(
                y[:], weights[:, t, e, :], picked, start=(i == 0), stop=(i == len(passes) - 1)
            )

        scaled = held.tile([M, V], F32, name="scaled")
        nc.vector.tensor_tensor(scaled[:], y[:], c_all[:], mybir.AluOpType.mult)
        nc.sync.dma_start(out, scaled[:])
